import numpy as np
import ml_dtypes


def mxq(x, axis, fmt="e4m3"):
    dtype, down = {"e4m3": (ml_dtypes.float8_e4m3fn, 7), "e5m2": (ml_dtypes.float8_e5m2, 14)}[fmt]
    v = np.moveaxis(np.asarray(x, np.float32).astype(ml_dtypes.bfloat16).astype(np.float64), axis, -1)
    blocks = v.reshape(v.shape[:-1] + (-1, 32))
    amax = np.abs(blocks).max(-1, keepdims=True)
    byte = np.maximum(np.where(amax > 0, np.frexp(amax)[1] - 1 + 127, 0) - down, 1)
    scale = np.exp2(byte - 127.0)
    codes = (blocks / scale).astype(np.float32).astype(dtype).astype(np.float64)
    return np.moveaxis((codes * scale).reshape(v.shape), -1, axis)


WIDE = False


def mx_kscale(k):
    if not WIDE:
        return np.ones(k)
    levels = np.array([10, -10, 5, -5, 0])
    if k % 512:
        return np.exp2(np.random.permutation(np.resize(levels, k // 32))).repeat(32)
    a = np.empty((k // 512, 16))
    for p in range(k // 512):
        a[p, :8] = np.random.permutation(np.resize(levels, 8))
        for g in range(8):
            far = levels[np.abs(levels - a[p, g]) >= 10]
            a[p, g + 8] = far[np.random.randint(len(far))]
    return np.exp2(a.ravel()).repeat(32)


BF16 = ml_dtypes.bfloat16


def bf(x):
    return np.asarray(x, np.float32).astype(BF16)


def f64(x):
    return np.asarray(x).astype(np.float64)


E2M1 = np.array([0.0, 0.5, 1.0, 1.5, 2.0, 3.0, 4.0, 6.0, -0.0, -0.5, -1.0, -1.5, -2.0, -3.0, -4.0, -6.0])


def pack_weight(w, fmt):
    k, n = w.shape
    w = f64(bf(w)).reshape(k // 32, 32, n)
    amax = np.abs(w).max(1)
    if fmt == "e4m3":
        byte = np.frexp(amax)[1] - 1 + 127 - 7
    else:
        mant, ex = np.frexp(amax / 6.0)
        byte = np.where(mant > 0.5, ex, ex - 1) + 127
    byte = np.clip(np.where(amax > 0, byte, 1), 1, 254)
    scaled = (w * np.exp2(127.0 - byte)[:, None, :]).reshape(k, n).astype(np.float32)
    by_word = np.ascontiguousarray(scaled.reshape(k // 512, 128, 4, n).transpose(0, 1, 3, 2))
    if fmt == "e4m3":
        words = by_word.astype(ml_dtypes.float8_e4m3fn).view(np.uint8)
    else:
        c = by_word.astype(ml_dtypes.float4_e2m1fn).view(np.uint8) & 0xF
        words = c[..., 0::2] | (c[..., 1::2] << 4)
    return np.ascontiguousarray(words), np.ascontiguousarray(byte.astype(np.uint8).reshape(k // 512, 16, n))


def unpack_weight(words, scales, fmt):
    g, p, n, _ = words.shape
    if fmt == "e4m3":
        vals = np.ascontiguousarray(words).view(ml_dtypes.float8_e4m3fn).astype(np.float64)
    else:
        nib = np.empty((g, p, n, 4), np.uint8)
        nib[..., 0::2] = words & 0xF
        nib[..., 1::2] = words >> 4
        vals = E2M1[nib]
    vals = vals * np.repeat(np.exp2(scales.astype(np.float64) - 127.0), 8, axis=1)[..., None]
    return vals.transpose(0, 1, 3, 2).reshape(g * 512, n)
def pack4(w):
    words, scales = pack_weight(w, "e2m1")
    return words.reshape(words.shape[0], 128, -1), scales


def unpack4(words, scales):
    return unpack_weight(words.reshape(words.shape[0], 128, -1, 2), scales, "e2m1")


M, H, T, N = 1024, 1024, 2048, 1536


def setup_inputs():
    s, t = mx_kscale(H), mx_kscale(T)
    u = np.concatenate([s, t])
    pre = np.random.standard_normal((M, H + T)) * u
    theta = (0.3 + 0.1 * np.random.standard_normal(H + T)) * u
    hot = np.random.standard_normal((N, H)) / np.sqrt(H) / s
    tail = np.random.standard_normal((T, N)) / np.sqrt(T) / t[:, None]
    tail_words, tail_scales = pack4(tail)
    return {"pre": bf(pre),
            "theta": bf(theta),
            "hot": bf(hot),
            "tail_words": tail_words,
            "tail_scales": tail_scales,
            "token_scale": bf(1 + 0.1 * np.random.standard_normal(M)),
            "b_dec": bf(0.3 * np.random.standard_normal(N))}


def reference(pre, theta, hot, tail_words, tail_scales, token_scale, b_dec):
    z = np.maximum(f64(pre) - f64(theta), 0)
    z_hot = mxq(z[:, :H], 1, "e4m3")
    z_tail = mxq(z[:, H:], 1, "e4m3")
    atoms = mxq(f64(hot), 1, "e4m3")
    y = (z_hot @ atoms.T) + (z_tail @ unpack4(tail_words, tail_scales))
    return y * f64(token_scale)[:, None] + f64(b_dec)

@@ -1,0 +1,362 @@
+from contextlib import ExitStack
+
+import concourse.mybir as mybir
+from concourse.masks import make_identity
+
+M, H, T, N = 1024, 1024, 2048, 1536
+FLOPS = 2 * M * (H + T) * N
+
+F32 = mybir.dt.float32
+BF16 = mybir.dt.bfloat16
+I32 = mybir.dt.int32
+U32 = mybir.dt.uint32
+U8 = mybir.dt.uint8
+FP8X4 = mybir.dt.float8_e4m3fn_x4
+FP4X4 = mybir.dt.float4_e2m1fn_x4
+ALU = mybir.AluOpType
+ACT = mybir.ActivationFunctionType
+
+P = 128
+TILES = M // P
+CHUNK = 512
+CHUNKS = N // CHUNK
+SPAN = 1024
+SPANS = (H + T) // SPAN
+HOT_SPAN = 0
+TAIL_SPANS = (1, 2)
+TAIL_PASSES = T // 512
+HOT_PASSES = H // 512
+
+
+def tile_relu_dictionary_readout_s1_kernel(
+    tc, pre, theta, hot, tail_words, tail_scales, token_scale, b_dec, out
+):
+    nc = tc.nc
+    pre_rows = pre.rearrange("(p m) k -> p m k", m=TILES)
+    out_rows = out.rearrange("(p m) n -> p m n", m=TILES)
+    hot_rows = hot.rearrange("(c h j p) k -> c h p j k", h=2, j=2, p=P)
+    tail_by_partition = tail_words.rearrange("g p n -> p g n")
+
+    with ExitStack() as ctx:
+        keep = ctx.enter_context(tc.tile_pool(name="keep", bufs=1))
+        stage = ctx.enter_context(tc.tile_pool(name="stage", bufs=4))
+        psum = ctx.enter_context(tc.psum_pool(name="psum", bufs=1))
+        ctx.enter_context(tc.manual_schedule())
+
+        pre_sb, hot_sb, tail_sb, theta_sb, bias_sb = {}, {}, {}, {}, {}
+        diff, z_t, z_mx, hot_sorted, hot_t, hot_mx, acc = {}, {}, {}, {}, {}, {}, {}
+
+        acc_bank = {}
+        free_banks = list(range(8))
+
+        def take_bank(name):
+            b = free_banks.pop(0)
+            return b, psum.tile([P, CHUNK], F32, name=name, tag="bank_%d" % b)
+
+        def load_pre(tiles, spans):
+            t = keep.tile([P, len(tiles), len(spans) * SPAN], BF16, name="pre_%d_%d" % (tiles[0], spans[0]))
+            nc.sync.dma_start(
+                out=t[:], in_=pre_rows[:, tiles[0] : tiles[-1] + 1, spans[0] * SPAN : (spans[-1] + 1) * SPAN]
+            )
+            for i, m in enumerate(tiles):
+                for j, s in enumerate(spans):
+                    pre_sb[m, s] = t[:, i, j * SPAN : (j + 1) * SPAN]
+
+        def load_tail(c):
+            t = keep.tile([P, TAIL_PASSES, 2 * CHUNK], U8, name="tail_%d" % c, align_bytes=64)
+            nc.sync.dma_start(
+                out=t[:].bitcast(I32), in_=tail_by_partition[:, :, 2 * CHUNK * c : 2 * CHUNK * (c + 1)].bitcast(I32)
+            )
+            tail_sb[c] = t
+
+        def load_hot(c):
+            for h in range(2):
+                t = keep.tile([P, 2, H], BF16, name="hot_%d_%d" % (c, h))
+                nc.sync.dma_start(out=t[:], in_=hot_rows[c, h])
+                hot_sb[c, h] = t
+
+        ident = keep.tile([P, P], F32, name="ident")
+        make_identity(nc, ident[:])
+        planes = {}
+
+        def clear_plane(chunks):
+            t = keep.tile([P, TAIL_PASSES, len(chunks) * CHUNK], U8, name="tail_plane_%d" % chunks[0], align_bytes=64)
+            nc.vector.memset(t[:].bitcast(I32), 0)
+            for i, c in enumerate(chunks):
+                planes[c] = t[:, :, i * CHUNK : (i + 1) * CHUNK]
+            return t
+
+        def load_plane(t, chunks):
+            cols = slice(chunks[0] * CHUNK, (chunks[-1] + 1) * CHUNK)
+            for q in range(4):
+                nc.sync.dma_start(
+                    out=t[32 * q : 32 * q + 4].bitcast(I32),
+                    in_=tail_scales[:, 4 * q : 4 * q + 4, cols].rearrange("g r n -> r g n").bitcast(I32),
+                )
+
+        first_plane = clear_plane([0])
+        later_planes = clear_plane([1, 2])
+        theta_cols = keep.tile([P, SPANS, 8], BF16, name="theta_cols")
+        gain_raw = keep.tile([P, TILES], BF16, name="gain_raw")
+        bias_cols = keep.tile([P, CHUNKS, 4], BF16, name="bias_cols")
+        nc.sync.dma_start(out=theta_cols[:], in_=theta.rearrange("(s p e) -> p s e", p=P, e=8))
+        load_pre([0], [1])
+        nc.sync.dma_start(out=gain_raw[:], in_=token_scale.rearrange("(p m) -> p m", m=TILES))
+        load_pre([0], [2])
+        load_plane(first_plane, [0])
+        load_tail(0)
+        nc.sync.dma_start(out=bias_cols[:], in_=b_dec.rearrange("(c p e) -> p c e", p=P, e=4))
+        load_pre([1], [1, 2])
+        load_plane(later_planes, [1, 2])
+        load_tail(1)
+        load_hot(0)
+        load_pre([0, 1], [0])
+        load_tail(2)
+        load_hot(1)
+        load_pre([2], [0, 1, 2])
+        load_hot(2)
+        for m in range(3, TILES):
+            load_pre([m], [0, 1, 2])
+
+        gain = keep.tile([P, TILES], F32, name="gain")
+        nc.scalar.activation(out=gain[:], in_=gain_raw[:], func=ACT.Identity)
+
+        def spread_theta(s, copy):
+            b, bank = take_bank("theta_bank_%d" % s)
+            words = theta_cols[:, s, :].bitcast(F32)
+            for w in range(4):
+                nc.tensor.transpose(bank[:, w * P : (w + 1) * P], words[:, w : w + 1].to_broadcast([P, P]), ident[:])
+            t = keep.tile([P, SPAN], BF16, name="theta_%d" % s)
+            copy(
+                out=t[:].bitcast(F32).rearrange("p (u n v) -> p u n v", u=2, v=2),
+                in_=bank[:].rearrange("p (v u n) -> p u n v", u=2, v=2),
+            )
+            theta_sb[s] = t
+            free_banks.append(b)
+
+        def spread_bias(c):
+            b, bank = take_bank("bias_bank_%d" % c)
+            words = bias_cols[:, c, :].bitcast(F32)
+            for u in range(2):
+                nc.tensor.transpose(bank[:, u * P : (u + 1) * P], words[:, u : u + 1].to_broadcast([P, P]), ident[:])
+            t = keep.tile([P, CHUNK], BF16, name="bias_%d" % c)
+            nc.scalar.copy(
+                out=t[:].bitcast(F32).rearrange("p (n u) -> p n u", u=2),
+                in_=bank[:, : 2 * P].rearrange("p (u n) -> p n u", u=2),
+            )
+            bias_sb[c] = t
+            free_banks.append(b)
+
+        def subtract(m, s):
+            t = stage.tile([P, SPAN], BF16, name="diff_%d_%d" % (m, s), tag="diff", bufs=8)
+            nc.vector.tensor_tensor(
+                out=t[:].rearrange("p (u w e) -> p u w e", u=2, e=2),
+                in0=pre_sb[m, s].rearrange("p (w u e) -> p u w e", u=2, e=2),
+                in1=theta_sb[s][:].rearrange("p (u w e) -> p u w e", u=2, e=2),
+                op=ALU.subtract,
+            )
+            diff[m, s] = t
+
+        def turn_z(m, s, on_vector=False):
+            b, bank = take_bank("z_bank_%d_%d" % (m, s))
+            words = diff[m, s][:].bitcast(F32)
+            for i in range(4):
+                nc.tensor.transpose(bank[:, i * P : (i + 1) * P], words[:, i * P : (i + 1) * P], ident[:])
+            t = stage.tile([P, SPAN], BF16, name="z_t_%d_%d" % (m, s), tag="z_t", bufs=4, align_bytes=64)
+            sorted_out = t[:].rearrange("p (r u e) -> p r u e", u=2, e=2)
+            halves = bank[:].bitcast(BF16).rearrange("p (u r e) -> p r u e", u=2, e=2)
+            if on_vector:
+                nc.vector.tensor_scalar_max(sorted_out, halves, 0.0)
+            else:
+                nc.scalar.activation(out=sorted_out, in_=halves, func=ACT.Relu)
+            z_t[m, s] = t
+            free_banks.append(b)
+
+        def quantize_z(m, s):
+            codes = keep.tile([P, 2 * P], U32, name="z_codes_%d_%d" % (m, s), align_bytes=64)
+            scales = keep.tile([P, 2 * P], U8, name="z_scales_%d_%d" % (m, s), align_bytes=64)
+            nc.vector.quantize_mx(out=codes[:].bitcast(FP8X4), scales=scales[:], in_=z_t[m, s][:])
+            z_mx[m, s] = (codes, scales)
+
+        def sort_hot(c, h, copy):
+            t = stage.tile([P, 2, 2, 2 * P], F32, name="hot_sorted_%d_%d" % (c, h), tag="hot_sorted", bufs=4)
+            copy(out=t[:], in_=hot_sb[c, h][:].bitcast(F32).rearrange("p j (w u) -> p j u w", u=2))
+            hot_sorted[c, h] = t
+
+        def turn_hot(c, h):
+            for g in range(HOT_PASSES):
+                if h == 0:
+                    hot_t[c, g] = stage.tile(
+                        [P, 4 * CHUNK], BF16, name="hot_t_%d_%d" % (c, g), tag="hot_t", bufs=4, align_bytes=64
+                    )
+                b, bank = take_bank("hot_bank_%d_%d_%d" % (c, h, g))
+                for u in range(2):
+                    for j in range(2):
+                        i = 2 * u + j
+                        nc.tensor.transpose(
+                            bank[:, i * P : (i + 1) * P], hot_sorted[c, h][:, j, u, g * P : (g + 1) * P], ident[:]
+                        )
+                nc.scalar.copy(
+                    out=hot_t[c, g][:, 2 * CHUNK * h : 2 * CHUNK * (h + 1)].bitcast(F32).rearrange("p (r u) -> p r u", u=2),
+                    in_=bank[:].rearrange("p (u r) -> p r u", u=2),
+                )
+                free_banks.append(b)
+
+        def quantize_hot(c, g):
+            codes = keep.tile([P, CHUNK], U32, name="hot_codes_%d_%d" % (c, g), align_bytes=64)
+            scales = keep.tile([P, CHUNK], U8, name="hot_scales_%d_%d" % (c, g), align_bytes=64)
+            nc.vector.quantize_mx(out=codes[:].bitcast(FP8X4), scales=scales[:], in_=hot_t[c, g][:])
+            hot_mx[c, g] = (codes, scales)
+
+        def tail_passes(m, c):
+            acc_bank[m, c], acc[m, c] = take_bank("acc_%d_%d" % (m, c))
+            for g in range(TAIL_PASSES):
+                codes, scales = z_mx[m, TAIL_SPANS[g // 2]]
+                cols = slice((g % 2) * P, (g % 2 + 1) * P)
+                nc.tensor.matmul_mx(
+                    out=acc[m, c][:],
+                    lhsT=codes[:, cols].bitcast(FP8X4),
+                    lhsT_scale=scales[:, cols],
+                    rhs=tail_sb[c][:, g, :].bitcast(FP4X4),
+                    rhs_scale=planes[c][:, g, :],
+                    start=(g == 0),
+                    stop=False,
+                )
+
+        def hot_passes(m, c):
+            codes, scales = z_mx[m, HOT_SPAN]
+            for g in range(HOT_PASSES):
+                cols = slice(g * P, (g + 1) * P)
+                nc.tensor.matmul_mx(
+                    out=acc[m, c][:],
+                    lhsT=codes[:, cols].bitcast(FP8X4),
+                    lhsT_scale=scales[:, cols],
+                    rhs=hot_mx[c, g][0][:].bitcast(FP8X4),
+                    rhs_scale=hot_mx[c, g][1][:],
+                    start=False,
+                    stop=(g == HOT_PASSES - 1),
+                )
+
+        def finish(m, c):
+            t = stage.tile([P, CHUNK], F32, name="result_%d_%d" % (m, c), tag="result", bufs=6)
+            nc.vector.scalar_tensor_tensor(
+                out=t[:], in0=acc[m, c][:], scalar=gain[:, m : m + 1], in1=bias_sb[c][:], op0=ALU.mult, op1=ALU.add
+            )
+            free_banks.append(acc_bank[m, c])
+            nc.sync.dma_start(out=out_rows[:, m, c * CHUNK : (c + 1) * CHUNK], in_=t[:])
+
+        def both(m, c):
+            tail_passes(m, c)
+            hot_passes(m, c)
+
+        vc = nc.vector.tensor_copy
+        sc = nc.scalar.copy
+        spread_theta(1, vc)
+        spread_theta(2, sc)
+        spread_theta(0, sc)
+        subtract(0, 1)
+        subtract(0, 2)
+        turn_z(0, 1, True)
+        turn_z(0, 2)
+        for c in range(CHUNKS):
+            spread_bias(c)
+        quantize_z(0, 1)
+        subtract(1, 1)
+        quantize_z(0, 2)
+        subtract(1, 2)
+        tail_passes(0, 0)
+        turn_z(1, 1, True)
+        turn_z(1, 2)
+        tail_passes(0, 1)
+        quantize_z(1, 1)
+        sort_hot(0, 0, vc)
+        quantize_z(1, 2)
+        sort_hot(0, 1, vc)
+        tail_passes(1, 0)
+        subtract(0, 0)
+        subtract(1, 0)
+        turn_hot(0, 0)
+        turn_hot(0, 1)
+        turn_z(0, 0, True)
+        turn_z(1, 0, True)
+        sort_hot(1, 0, sc)
+        sort_hot(1, 1, sc)
+        quantize_hot(0, 0)
+        quantize_z(0, 0)
+        quantize_hot(0, 1)
+        quantize_z(1, 0)
+        tail_passes(1, 1)
+        tail_passes(0, 2)
+        hot_passes(0, 0)
+        hot_passes(1, 0)
+        finish(0, 0)
+        subtract(2, 1)
+        subtract(2, 2)
+        turn_hot(1, 0)
+        turn_hot(1, 1)
+        finish(1, 0)
+        turn_z(2, 1, True)
+        turn_z(2, 2)
+        sort_hot(2, 0, sc)
+        sort_hot(2, 1, sc)
+        quantize_hot(1, 0)
+        quantize_hot(1, 1)
+        tail_passes(1, 2)
+        quantize_z(2, 1)
+        quantize_z(2, 2)
+        subtract(2, 0)
+        hot_passes(0, 1)
+        hot_passes(1, 1)
+        tail_passes(2, 0)
+        finish(0, 1)
+        finish(1, 1)
+        subtract(3, 1)
+        subtract(3, 2)
+        turn_z(2, 0, True)
+        turn_hot(2, 0)
+        turn_hot(2, 1)
+        subtract(3, 0)
+        quantize_z(2, 0)
+        subtract(4, 1)
+        subtract(4, 2)
+        tail_passes(2, 1)
+        hot_passes(2, 0)
+        hot_passes(2, 1)
+        quantize_hot(2, 0)
+        quantize_hot(2, 1)
+        finish(2, 0)
+        for s in (1, 2, 0):
+            turn_z(3, s)
+        finish(2, 1)
+        hot_passes(0, 2)
+        hot_passes(1, 2)
+        both(2, 2)
+        quantize_z(3, 1)
+        subtract(4, 0)
+        finish(0, 2)
+        quantize_z(3, 2)
+        finish(1, 2)
+        quantize_z(3, 0)
+
+        for m in range(3, TILES):
+            turn = m + 1 < TILES
+            ahead = m + 2 < TILES
+            if turn:
+                for s in (1, 2, 0):
+                    turn_z(m + 1, s)
+            finish(m - 1, 2)
+            both(m, 0)
+            for s in TAIL_SPANS:
+                if ahead:
+                    subtract(m + 2, s)
+                if turn:
+                    quantize_z(m + 1, s)
+            finish(m, 0)
+            both(m, 1)
+            if turn:
+                quantize_z(m + 1, HOT_SPAN)
+            if ahead:
+                subtract(m + 2, HOT_SPAN)
+            finish(m, 1)
+            both(m, 2)
+        finish(TILES - 1, 2)

@@ -94,26 +94,28 @@ def tile_relu_dictionary_readout_s1_kernel(
                     in_=tail_scales[:, 4 * q : 4 * q + 4, cols].rearrange("g r n -> r g n").bitcast(I32),
                 )
 
-        first_plane = clear_plane([0])
-        later_planes = clear_plane([1, 2])
+        plane_tiles = [clear_plane([c]) for c in range(CHUNKS)]
         theta_cols = keep.tile([P, SPANS, 8], BF16, name="theta_cols")
         gain_raw = keep.tile([P, TILES], BF16, name="gain_raw")
         bias_cols = keep.tile([P, CHUNKS, 4], BF16, name="bias_cols")
         nc.sync.dma_start(out=theta_cols[:], in_=theta.rearrange("(s p e) -> p s e", p=P, e=8))
         load_pre([0], [1])
         nc.sync.dma_start(out=gain_raw[:], in_=token_scale.rearrange("(p m) -> p m", m=TILES))
-        load_pre([0], [2])
-        load_plane(first_plane, [0])
-        load_tail(0)
         nc.sync.dma_start(out=bias_cols[:], in_=b_dec.rearrange("(c p e) -> p c e", p=P, e=4))
-        load_pre([1], [1, 2])
-        load_plane(later_planes, [1, 2])
-        load_tail(1)
+        load_pre([0], [2])
+        load_pre([0], [0])
         load_hot(0)
-        load_pre([0, 1], [0])
-        load_tail(2)
+        load_pre([1], [1, 2])
+        load_pre([1], [0])
+        load_plane(plane_tiles[0], [0])
+        load_tail(0)
+        load_plane(plane_tiles[1], [1])
+        load_tail(1)
         load_hot(1)
-        load_pre([2], [0, 1, 2])
+        load_pre([2], [1, 2])
+        load_pre([2], [0])
+        load_plane(plane_tiles[2], [2])
+        load_tail(2)
         load_hot(2)
         for m in range(3, TILES):
             load_pre([m], [0, 1, 2])
@@ -183,7 +185,7 @@ def tile_relu_dictionary_readout_s1_kernel(
             copy(out=t[:], in_=hot_sb[c, h][:].bitcast(F32).rearrange("p j (w u) -> p j u w", u=2))
             hot_sorted[c, h] = t
 
-        def turn_hot(c, h):
+        def turn_hot(c, h, copies=None):
             for g in range(HOT_PASSES):
                 if h == 0:
                     hot_t[c, g] = stage.tile(
@@ -193,10 +195,12 @@ def tile_relu_dictionary_readout_s1_kernel(
                 for u in range(2):
                     for j in range(2):
                         i = 2 * u + j
-                        nc.tensor.transpose(
-                            bank[:, i * P : (i + 1) * P], hot_sorted[c, h][:, j, u, g * P : (g + 1) * P], ident[:]
-                        )
-                nc.scalar.copy(
+                        if (c, h) in hot_sorted:
+                            words = hot_sorted[c, h][:, j, u, g * P : (g + 1) * P]
+                        else:
+                            words = hot_sb[c, h][:, j, :].bitcast(F32)[:, 2 * P * g + u : 2 * P * (g + 1) : 2]
+                        nc.tensor.transpose(bank[:, i * P : (i + 1) * P], words, ident[:])
+                (copies[g] if copies else nc.scalar.copy)(
                     out=hot_t[c, g][:, 2 * CHUNK * h : 2 * CHUNK * (h + 1)].bitcast(F32).rearrange("p (r u) -> p r u", u=2),
                     in_=bank[:].rearrange("p (u r) -> p r u", u=2),
                 )
@@ -223,6 +227,21 @@ def tile_relu_dictionary_readout_s1_kernel(
                     stop=False,
                 )
 
+        def warm_up(passes):
+            b, bank = take_bank("warm_bank_%d" % len(hot_t))
+            codes, scales = z_mx[0, 1]
+            for i in range(passes):
+                nc.tensor.matmul_mx(
+                    out=bank[:, : 2 * P],
+                    lhsT=codes[:, :P].bitcast(FP8X4),
+                    lhsT_scale=scales[:, :P],
+                    rhs=codes[:].bitcast(FP8X4),
+                    rhs_scale=scales[:],
+                    start=True,
+                    stop=True,
+                )
+            free_banks.append(b)
+
         def hot_passes(m, c):
             codes, scales = z_mx[m, HOT_SPAN]
             for g in range(HOT_PASSES):
@@ -237,13 +256,21 @@ def tile_relu_dictionary_readout_s1_kernel(
                     stop=(g == HOT_PASSES - 1),
                 )
 
-        def finish(m, c):
-            t = stage.tile([P, CHUNK], F32, name="result_%d_%d" % (m, c), tag="result", bufs=6)
-            nc.vector.scalar_tensor_tensor(
-                out=t[:], in0=acc[m, c][:], scalar=gain[:, m : m + 1], in1=bias_sb[c][:], op0=ALU.mult, op1=ALU.add
-            )
+        def finish(m, c, pieces=1):
+            width = CHUNK // pieces
+            for i in range(pieces):
+                cols = slice(i * width, (i + 1) * width)
+                t = stage.tile([P, width], F32, name="result_%d_%d_%d" % (m, c, i), tag="result", bufs=8)
+                nc.vector.scalar_tensor_tensor(
+                    out=t[:],
+                    in0=acc[m, c][:, cols],
+                    scalar=gain[:, m : m + 1],
+                    in1=bias_sb[c][:, cols],
+                    op0=ALU.mult,
+                    op1=ALU.add,
+                )
+                nc.sync.dma_start(out=out_rows[:, m, c * CHUNK + i * width : c * CHUNK + (i + 1) * width], in_=t[:])
             free_banks.append(acc_bank[m, c])
-            nc.sync.dma_start(out=out_rows[:, m, c * CHUNK : (c + 1) * CHUNK], in_=t[:])
 
         def both(m, c):
             tail_passes(m, c)
@@ -254,74 +281,70 @@ def tile_relu_dictionary_readout_s1_kernel(
         spread_theta(1, vc)
         spread_theta(2, sc)
         spread_theta(0, sc)
-        subtract(0, 1)
-        subtract(0, 2)
-        turn_z(0, 1, True)
-        turn_z(0, 2)
         for c in range(CHUNKS):
             spread_bias(c)
-        quantize_z(0, 1)
-        subtract(1, 1)
-        quantize_z(0, 2)
-        subtract(1, 2)
-        tail_passes(0, 0)
-        turn_z(1, 1, True)
-        turn_z(1, 2)
-        tail_passes(0, 1)
-        quantize_z(1, 1)
-        sort_hot(0, 0, vc)
-        quantize_z(1, 2)
-        sort_hot(0, 1, vc)
-        tail_passes(1, 0)
+        subtract(0, 1)
+        subtract(0, 2)
         subtract(0, 0)
-        subtract(1, 0)
-        turn_hot(0, 0)
+        turn_z(0, 1)
+        turn_z(0, 2)
+        turn_z(0, 0)
+        sort_hot(0, 0, vc)
+        quantize_z(0, 1)
+        sort_hot(0, 1, vc)
+        turn_hot(0, 0, [vc, sc])
+        warm_up(4)
         turn_hot(0, 1)
-        turn_z(0, 0, True)
-        turn_z(1, 0, True)
-        sort_hot(1, 0, sc)
-        sort_hot(1, 1, sc)
-        quantize_hot(0, 0)
+        quantize_z(0, 2)
+        subtract(1, 1)
+        subtract(1, 2)
         quantize_z(0, 0)
+        subtract(1, 0)
+        turn_z(1, 1)
+        turn_z(1, 2, True)
+        warm_up(2)
+        turn_z(1, 0)
+        quantize_hot(0, 0)
         quantize_hot(0, 1)
+        both(0, 0)
+        quantize_z(1, 1)
+        quantize_z(1, 2)
         quantize_z(1, 0)
-        tail_passes(1, 1)
-        tail_passes(0, 2)
-        hot_passes(0, 0)
-        hot_passes(1, 0)
         finish(0, 0)
-        subtract(2, 1)
-        subtract(2, 2)
+        both(1, 0)
+        sort_hot(1, 0, vc)
+        finish(1, 0)
+        sort_hot(1, 1, vc)
+        tail_passes(0, 1)
         turn_hot(1, 0)
         turn_hot(1, 1)
-        finish(1, 0)
-        turn_z(2, 1, True)
-        turn_z(2, 2)
-        sort_hot(2, 0, sc)
-        sort_hot(2, 1, sc)
+        subtract(2, 1)
+        subtract(2, 2)
+        subtract(2, 0)
+        tail_passes(1, 1)
         quantize_hot(1, 0)
         quantize_hot(1, 1)
-        tail_passes(1, 2)
-        quantize_z(2, 1)
-        quantize_z(2, 2)
-        subtract(2, 0)
+        turn_z(2, 1)
+        turn_z(2, 2)
+        turn_z(2, 0, True)
+        tail_passes(0, 2)
         hot_passes(0, 1)
         hot_passes(1, 1)
-        tail_passes(2, 0)
+        tail_passes(1, 2)
+        quantize_z(2, 1)
+        sort_hot(2, 0, vc)
+        quantize_z(2, 2)
+        sort_hot(2, 1, vc)
+        quantize_z(2, 0)
         finish(0, 1)
         finish(1, 1)
-        subtract(3, 1)
-        subtract(3, 2)
-        turn_z(2, 0, True)
         turn_hot(2, 0)
         turn_hot(2, 1)
+        subtract(3, 1)
+        subtract(3, 2)
         subtract(3, 0)
-        quantize_z(2, 0)
-        subtract(4, 1)
-        subtract(4, 2)
-        tail_passes(2, 1)
-        hot_passes(2, 0)
-        hot_passes(2, 1)
+        both(2, 0)
+        both(2, 1)
         quantize_hot(2, 0)
         quantize_hot(2, 1)
         finish(2, 0)
@@ -331,10 +354,12 @@ def tile_relu_dictionary_readout_s1_kernel(
         hot_passes(0, 2)
         hot_passes(1, 2)
         both(2, 2)
+        subtract(4, 1)
         quantize_z(3, 1)
-        subtract(4, 0)
+        subtract(4, 2)
         finish(0, 2)
         quantize_z(3, 2)
+        subtract(4, 0)
         finish(1, 2)
         quantize_z(3, 0)
 
@@ -359,4 +384,4 @@ def tile_relu_dictionary_readout_s1_kernel(
                 subtract(m + 2, HOT_SPAN)
             finish(m, 1)
             both(m, 2)
-        finish(TILES - 1, 2)
+        finish(TILES - 1, 2, 2)

@@ -17,6 +17,9 @@ ALU = mybir.AluOpType
 ACT = mybir.ActivationFunctionType
 
 P = 128
+BANKS = 8
+QUAD = 32
+QUADS = P // QUAD
 TILES = M // P
 CHUNK = 512
 CHUNKS = N // CHUNK
@@ -24,14 +27,22 @@ SPAN = 1024
 SPANS = (H + T) // SPAN
 HOT_SPAN = 0
 TAIL_SPANS = (1, 2)
-TAIL_PASSES = T // 512
+SPAN_ORDER = (1, 2, 0)
 HOT_PASSES = H // 512
+TAIL_PASSES = T // 512
+PASSES = HOT_PASSES + TAIL_PASSES
+MX_ALIGN = 64
+
+DIFF_BUFS = 2 * SPANS
+TURNED_BUFS = SPANS + 1
+RESULT_BUFS = 9
 
 
 def tile_relu_dictionary_readout_s1_kernel(
     tc, pre, theta, hot, tail_words, tail_scales, token_scale, b_dec, out
 ):
     nc = tc.nc
+    vector_copy, scalar_copy = nc.vector.tensor_copy, nc.scalar.copy
     pre_rows = pre.rearrange("(p m) k -> p m k", m=TILES)
     out_rows = out.rearrange("(p m) n -> p m n", m=TILES)
     hot_rows = hot.rearrange("(c h j p) k -> c h p j k", h=2, j=2, p=P)
@@ -39,35 +50,38 @@ def tile_relu_dictionary_readout_s1_kernel(
 
     with ExitStack() as ctx:
         keep = ctx.enter_context(tc.tile_pool(name="keep", bufs=1))
-        stage = ctx.enter_context(tc.tile_pool(name="stage", bufs=4))
+        stage = ctx.enter_context(tc.tile_pool(name="stage", bufs=2))
         psum = ctx.enter_context(tc.psum_pool(name="psum", bufs=1))
         ctx.enter_context(tc.manual_schedule())
 
-        pre_sb, hot_sb, tail_sb, theta_sb, bias_sb = {}, {}, {}, {}, {}
-        diff, z_t, z_mx, hot_sorted, hot_t, hot_mx, acc = {}, {}, {}, {}, {}, {}, {}
+        pre_sb, diff, z_turned, z_mx = {}, {}, {}, {}
+        pre_quad, diff_quad = {}, {}
+        z_quad = {}
+        hot_sb, hot_sorted = {}, {}
+        hot_turned, hot_mx = {}, {}
+        tail_sb, bias_sb = {}, {}
+        theta_sb = {}
+        open_groups = {}
 
-        acc_bank = {}
-        free_banks = list(range(8))
+        free_banks = list(range(BANKS))
 
         def take_bank(name):
             b = free_banks.pop(0)
             return b, psum.tile([P, CHUNK], F32, name=name, tag="bank_%d" % b)
 
-        def load_pre(tiles, spans):
-            t = keep.tile([P, len(tiles), len(spans) * SPAN], BF16, name="pre_%d_%d" % (tiles[0], spans[0]))
-            nc.sync.dma_start(
-                out=t[:], in_=pre_rows[:, tiles[0] : tiles[-1] + 1, spans[0] * SPAN : (spans[-1] + 1) * SPAN]
-            )
-            for i, m in enumerate(tiles):
-                for j, s in enumerate(spans):
-                    pre_sb[m, s] = t[:, i, j * SPAN : (j + 1) * SPAN]
+        def load_pre(m, spans):
+            t = keep.tile([P, len(spans) * SPAN], BF16, name="pre_%d_%d" % (m, spans[0]))
+            nc.sync.dma_start(out=t[:], in_=pre_rows[:, m, spans[0] * SPAN : (spans[-1] + 1) * SPAN])
+            for i, s in enumerate(spans):
+                pre_sb[m, s] = t[:, i * SPAN : (i + 1) * SPAN]
 
-        def load_tail(c):
-            t = keep.tile([P, TAIL_PASSES, 2 * CHUNK], U8, name="tail_%d" % c, align_bytes=64)
-            nc.sync.dma_start(
-                out=t[:].bitcast(I32), in_=tail_by_partition[:, :, 2 * CHUNK * c : 2 * CHUNK * (c + 1)].bitcast(I32)
-            )
-            tail_sb[c] = t
+        def load_pre_quad(m, h):
+            rows = pre_rows[:, m, :].rearrange("(a i) (g q k) -> q a i g k", i=QUAD, q=QUADS, k=P)
+            t = keep.tile([P, 2, PASSES, P], BF16, name="pre_quad_%d_%d" % (m, h))
+            for a in range(2):
+                for q in (0, 2, 1, 3):
+                    nc.sync.dma_start(out=t[QUAD * q : QUAD * (q + 1), a], in_=rows[q, 2 * h + a])
+            pre_quad[m, h] = t
 
         def load_hot(c):
             for h in range(2):
@@ -75,59 +89,26 @@ def tile_relu_dictionary_readout_s1_kernel(
                 nc.sync.dma_start(out=t[:], in_=hot_rows[c, h])
                 hot_sb[c, h] = t
 
-        ident = keep.tile([P, P], F32, name="ident")
-        make_identity(nc, ident[:])
-        planes = {}
-
-        def clear_plane(chunks):
-            t = keep.tile([P, TAIL_PASSES, len(chunks) * CHUNK], U8, name="tail_plane_%d" % chunks[0], align_bytes=64)
-            nc.vector.memset(t[:].bitcast(I32), 0)
-            for i, c in enumerate(chunks):
-                planes[c] = t[:, :, i * CHUNK : (i + 1) * CHUNK]
-            return t
-
-        def load_plane(t, chunks):
-            cols = slice(chunks[0] * CHUNK, (chunks[-1] + 1) * CHUNK)
-            for q in range(4):
+        def load_tail(c):
+            for q in range(QUADS):
                 nc.sync.dma_start(
-                    out=t[32 * q : 32 * q + 4].bitcast(I32),
-                    in_=tail_scales[:, 4 * q : 4 * q + 4, cols].rearrange("g r n -> r g n").bitcast(I32),
+                    out=tail_planes[c][QUAD * q : QUAD * q + 4].bitcast(I32),
+                    in_=tail_scales[:, 4 * q : 4 * q + 4, c * CHUNK : (c + 1) * CHUNK]
+                    .rearrange("g r n -> r g n")
+                    .bitcast(I32),
                 )
-
-        plane_tiles = [clear_plane([c]) for c in range(CHUNKS)]
-        theta_cols = keep.tile([P, SPANS, 8], BF16, name="theta_cols")
-        gain_raw = keep.tile([P, TILES], BF16, name="gain_raw")
-        bias_cols = keep.tile([P, CHUNKS, 4], BF16, name="bias_cols")
-        nc.sync.dma_start(out=theta_cols[:], in_=theta.rearrange("(s p e) -> p s e", p=P, e=8))
-        load_pre([0], [1])
-        nc.sync.dma_start(out=gain_raw[:], in_=token_scale.rearrange("(p m) -> p m", m=TILES))
-        nc.sync.dma_start(out=bias_cols[:], in_=b_dec.rearrange("(c p e) -> p c e", p=P, e=4))
-        load_pre([0], [2])
-        load_pre([0], [0])
-        load_hot(0)
-        load_pre([1], [1, 2])
-        load_pre([1], [0])
-        load_plane(plane_tiles[0], [0])
-        load_tail(0)
-        load_plane(plane_tiles[1], [1])
-        load_tail(1)
-        load_hot(1)
-        load_pre([2], [1, 2])
-        load_pre([2], [0])
-        load_plane(plane_tiles[2], [2])
-        load_tail(2)
-        load_hot(2)
-        for m in range(3, TILES):
-            load_pre([m], [0, 1, 2])
-
-        gain = keep.tile([P, TILES], F32, name="gain")
-        nc.scalar.activation(out=gain[:], in_=gain_raw[:], func=ACT.Identity)
+            t = keep.tile([P, TAIL_PASSES, 2 * CHUNK], U8, name="tail_%d" % c, align_bytes=MX_ALIGN)
+            nc.sync.dma_start(
+                out=t[:].bitcast(I32),
+                in_=tail_by_partition[:, :, 2 * CHUNK * c : 2 * CHUNK * (c + 1)].bitcast(I32),
+            )
+            tail_sb[c] = t
 
         def spread_theta(s, copy):
             b, bank = take_bank("theta_bank_%d" % s)
-            words = theta_cols[:, s, :].bitcast(F32)
+            pairs = theta_cols[:, s, :].bitcast(F32)
             for w in range(4):
-                nc.tensor.transpose(bank[:, w * P : (w + 1) * P], words[:, w : w + 1].to_broadcast([P, P]), ident[:])
+                nc.tensor.transpose(bank[:, w * P : (w + 1) * P], pairs[:, w : w + 1].to_broadcast([P, P]), ident[:])
             t = keep.tile([P, SPAN], BF16, name="theta_%d" % s)
             copy(
                 out=t[:].bitcast(F32).rearrange("p (u n v) -> p u n v", u=2, v=2),
@@ -138,19 +119,27 @@ def tile_relu_dictionary_readout_s1_kernel(
 
         def spread_bias(c):
             b, bank = take_bank("bias_bank_%d" % c)
-            words = bias_cols[:, c, :].bitcast(F32)
-            for u in range(2):
-                nc.tensor.transpose(bank[:, u * P : (u + 1) * P], words[:, u : u + 1].to_broadcast([P, P]), ident[:])
+            pairs = bias_cols[:, c, :].bitcast(F32)
+            for w in range(2):
+                nc.tensor.transpose(bank[:, w * P : (w + 1) * P], pairs[:, w : w + 1].to_broadcast([P, P]), ident[:])
             t = keep.tile([P, CHUNK], BF16, name="bias_%d" % c)
-            nc.scalar.copy(
-                out=t[:].bitcast(F32).rearrange("p (n u) -> p n u", u=2),
-                in_=bank[:, : 2 * P].rearrange("p (u n) -> p n u", u=2),
+            scalar_copy(
+                out=t[:].bitcast(F32).rearrange("p (n w) -> p n w", w=2),
+                in_=bank[:, : 2 * P].rearrange("p (w n) -> p n w", w=2),
             )
             bias_sb[c] = t
             free_banks.append(b)
 
+        def gather_theta_quad():
+            for q in range(QUADS):
+                rows = slice(QUAD * q, QUAD * (q + 1))
+                for s in range(SPANS):
+                    pairs = theta_sb[s][rows].bitcast(F32).rearrange("p (u g q j) -> p u g q j", u=2, g=2, q=QUADS)
+                    scalar_copy(out=theta_quad[rows, :, 0, 2 * s : 2 * s + 2, :], in_=pairs[:, :, :, q, :])
+            scalar_copy(out=theta_quad[:, :, 1], in_=theta_quad[:, :, 0])
+
         def subtract(m, s):
-            t = stage.tile([P, SPAN], BF16, name="diff_%d_%d" % (m, s), tag="diff", bufs=8)
+            t = stage.tile([P, SPAN], BF16, name="diff_%d_%d" % (m, s), tag="diff", bufs=DIFF_BUFS)
             nc.vector.tensor_tensor(
                 out=t[:].rearrange("p (u w e) -> p u w e", u=2, e=2),
                 in0=pre_sb[m, s].rearrange("p (w u e) -> p u w e", u=2, e=2),
@@ -159,77 +148,148 @@ def tile_relu_dictionary_readout_s1_kernel(
             )
             diff[m, s] = t
 
-        def turn_z(m, s, on_vector=False):
+        def relu_on_scalar(target, source):
+            nc.scalar.activation(out=target, in_=source, func=ACT.Relu)
+
+        def relu_on_vector(target, source):
+            nc.vector.tensor_scalar_max(target, source, 0.0)
+
+        def turn_z(m, s, relu=relu_on_scalar):
             b, bank = take_bank("z_bank_%d_%d" % (m, s))
-            words = diff[m, s][:].bitcast(F32)
+            pairs = diff[m, s][:].bitcast(F32)
             for i in range(4):
-                nc.tensor.transpose(bank[:, i * P : (i + 1) * P], words[:, i * P : (i + 1) * P], ident[:])
-            t = stage.tile([P, SPAN], BF16, name="z_t_%d_%d" % (m, s), tag="z_t", bufs=4, align_bytes=64)
-            sorted_out = t[:].rearrange("p (r u e) -> p r u e", u=2, e=2)
-            halves = bank[:].bitcast(BF16).rearrange("p (u r e) -> p r u e", u=2, e=2)
-            if on_vector:
-                nc.vector.tensor_scalar_max(sorted_out, halves, 0.0)
-            else:
-                nc.scalar.activation(out=sorted_out, in_=halves, func=ACT.Relu)
-            z_t[m, s] = t
+                nc.tensor.transpose(bank[:, i * P : (i + 1) * P], pairs[:, i * P : (i + 1) * P], ident[:])
+            t = stage.tile(
+                [P, SPAN], BF16, name="z_turned_%d_%d" % (m, s), tag="z_turned", bufs=TURNED_BUFS, align_bytes=MX_ALIGN
+            )
+            relu(
+                t[:].rearrange("p (r u e) -> p r u e", u=2, e=2),
+                bank[:].bitcast(BF16).rearrange("p (u r e) -> p r u e", u=2, e=2),
+            )
+            z_turned[m, s] = t[:]
             free_banks.append(b)
 
         def quantize_z(m, s):
-            codes = keep.tile([P, 2 * P], U32, name="z_codes_%d_%d" % (m, s), align_bytes=64)
-            scales = keep.tile([P, 2 * P], U8, name="z_scales_%d_%d" % (m, s), align_bytes=64)
-            nc.vector.quantize_mx(out=codes[:].bitcast(FP8X4), scales=scales[:], in_=z_t[m, s][:])
+            codes = keep.tile([P, 2 * P], U32, name="z_codes_%d_%d" % (m, s), align_bytes=MX_ALIGN)
+            scales = keep.tile([P, 2 * P], U8, name="z_scales_%d_%d" % (m, s), align_bytes=MX_ALIGN)
+            nc.vector.quantize_mx(out=codes[:].bitcast(FP8X4), scales=scales[:], in_=z_turned[m, s])
             z_mx[m, s] = (codes, scales)
 
-        def sort_hot(c, h, copy):
-            t = stage.tile([P, 2, 2, 2 * P], F32, name="hot_sorted_%d_%d" % (c, h), tag="hot_sorted", bufs=4)
-            copy(out=t[:], in_=hot_sb[c, h][:].bitcast(F32).rearrange("p j (w u) -> p j u w", u=2))
+        def subtract_quad(m, h):
+            t = stage.tile(
+                [P, 2 * PASSES * P], BF16, name="diff_quad_%d_%d" % (m, h), tag="diff_quad", align_bytes=MX_ALIGN
+            )
+            nc.vector.tensor_tensor(
+                out=t[:].rearrange("p (u a w e) -> p u a w e", u=2, a=2, e=2),
+                in0=pre_quad[m, h][:].rearrange("p a g (j u e) -> p u a (g j) e", u=2, e=2),
+                in1=theta_quad[:].bitcast(BF16).rearrange("p u a g (j e) -> p u a (g j) e", e=2),
+                op=ALU.subtract,
+            )
+            diff_quad[m, h] = t
+
+        def turn_quad(m, h):
+            blocks = stage.tile(
+                [P, PASSES * P], F32, name="blocks_%d_%d" % (m, h), tag="blocks", align_bytes=MX_ALIGN
+            )
+            nc.vector.transpose(blocks[:], diff_quad[m, h][:].bitcast(F32))
+            if h == 0:
+                z_quad[m] = stage.tile(
+                    [P, SPANS * SPAN], BF16, name="z_quad_%d" % m, tag="z_quad", align_bytes=MX_ALIGN
+                )
+                for s in range(SPANS):
+                    z_turned[m, s] = z_quad[m][:, s * SPAN : (s + 1) * SPAN]
+            by_token_group = z_quad[m][:].rearrange("p (g a i u e) -> p a g i u e", a=QUADS, i=QUAD, u=2, e=2)
+            relu_on_scalar(
+                by_token_group[:, 2 * h : 2 * h + 2],
+                blocks[:].bitcast(BF16).rearrange("p (u a g i e) -> p a g i u e", u=2, a=2, i=QUAD, e=2),
+            )
+
+        def sort_hot(c, h):
+            t = stage.tile([P, 2, 2, 2 * P], F32, name="hot_sorted_%d_%d" % (c, h), tag="hot_sorted")
+            vector_copy(out=t[:], in_=hot_sb[c, h][:].bitcast(F32).rearrange("p j (w u) -> p j u w", u=2))
             hot_sorted[c, h] = t
 
-        def turn_hot(c, h, copies=None):
+        def turn_hot(c, h, copies=(scalar_copy, scalar_copy)):
             for g in range(HOT_PASSES):
                 if h == 0:
-                    hot_t[c, g] = stage.tile(
-                        [P, 4 * CHUNK], BF16, name="hot_t_%d_%d" % (c, g), tag="hot_t", bufs=4, align_bytes=64
+                    hot_turned[c, g] = stage.tile(
+                        [P, 4 * CHUNK], BF16, name="hot_turned_%d_%d" % (c, g), tag="hot_turned", align_bytes=MX_ALIGN
                     )
                 b, bank = take_bank("hot_bank_%d_%d_%d" % (c, h, g))
                 for u in range(2):
                     for j in range(2):
                         i = 2 * u + j
-                        if (c, h) in hot_sorted:
-                            words = hot_sorted[c, h][:, j, u, g * P : (g + 1) * P]
-                        else:
-                            words = hot_sb[c, h][:, j, :].bitcast(F32)[:, 2 * P * g + u : 2 * P * (g + 1) : 2]
-                        nc.tensor.transpose(bank[:, i * P : (i + 1) * P], words, ident[:])
-                (copies[g] if copies else nc.scalar.copy)(
-                    out=hot_t[c, g][:, 2 * CHUNK * h : 2 * CHUNK * (h + 1)].bitcast(F32).rearrange("p (r u) -> p r u", u=2),
+                        nc.tensor.transpose(
+                            bank[:, i * P : (i + 1) * P], hot_sorted[c, h][:, j, u, g * P : (g + 1) * P], ident[:]
+                        )
+                half = hot_turned[c, g][:, 2 * CHUNK * h : 2 * CHUNK * (h + 1)]
+                copies[g](
+                    out=half.bitcast(F32).rearrange("p (r u) -> p r u", u=2),
                     in_=bank[:].rearrange("p (u r) -> p r u", u=2),
                 )
                 free_banks.append(b)
 
-        def quantize_hot(c, g):
-            codes = keep.tile([P, CHUNK], U32, name="hot_codes_%d_%d" % (c, g), align_bytes=64)
-            scales = keep.tile([P, CHUNK], U8, name="hot_scales_%d_%d" % (c, g), align_bytes=64)
-            nc.vector.quantize_mx(out=codes[:].bitcast(FP8X4), scales=scales[:], in_=hot_t[c, g][:])
-            hot_mx[c, g] = (codes, scales)
+        def quantize_hot(c):
+            for g in range(HOT_PASSES):
+                codes = keep.tile([P, CHUNK], U32, name="hot_codes_%d_%d" % (c, g), align_bytes=MX_ALIGN)
+                scales = keep.tile([P, CHUNK], U8, name="hot_scales_%d_%d" % (c, g), align_bytes=MX_ALIGN)
+                nc.vector.quantize_mx(out=codes[:].bitcast(FP8X4), scales=scales[:], in_=hot_turned[c, g][:])
+                hot_mx[c, g] = (codes, scales)
 
-        def tail_passes(m, c):
-            acc_bank[m, c], acc[m, c] = take_bank("acc_%d_%d" % (m, c))
+        def tail_passes(m, c, first=0, width=CHUNK):
+            open_groups[m, c * CHUNK + first] = take_bank("sums_%d_%d" % (m, c * CHUNK + first))
+            bank = open_groups[m, c * CHUNK + first][1]
             for g in range(TAIL_PASSES):
                 codes, scales = z_mx[m, TAIL_SPANS[g // 2]]
-                cols = slice((g % 2) * P, (g % 2 + 1) * P)
+                tokens = slice((g % 2) * P, (g % 2 + 1) * P)
                 nc.tensor.matmul_mx(
-                    out=acc[m, c][:],
-                    lhsT=codes[:, cols].bitcast(FP8X4),
-                    lhsT_scale=scales[:, cols],
-                    rhs=tail_sb[c][:, g, :].bitcast(FP4X4),
-                    rhs_scale=planes[c][:, g, :],
+                    out=bank[:, :width],
+                    lhsT=codes[:, tokens].bitcast(FP8X4),
+                    lhsT_scale=scales[:, tokens],
+                    rhs=tail_sb[c][:, g, 2 * first : 2 * (first + width)].bitcast(FP4X4),
+                    rhs_scale=tail_planes[c][:, g, first : first + width],
                     start=(g == 0),
                     stop=False,
                 )
 
-        def warm_up(passes):
-            b, bank = take_bank("warm_bank_%d" % len(hot_t))
-            codes, scales = z_mx[0, 1]
+        def hot_passes(m, c, first=0, width=CHUNK):
+            bank = open_groups[m, c * CHUNK + first][1]
+            codes, scales = z_mx[m, HOT_SPAN]
+            for g in range(HOT_PASSES):
+                tokens = slice(g * P, (g + 1) * P)
+                hot_codes, hot_scales = hot_mx[c, g]
+                nc.tensor.matmul_mx(
+                    out=bank[:, :width],
+                    lhsT=codes[:, tokens].bitcast(FP8X4),
+                    lhsT_scale=scales[:, tokens],
+                    rhs=hot_codes[:, first : first + width].bitcast(FP8X4),
+                    rhs_scale=hot_scales[:, first : first + width],
+                    start=False,
+                    stop=(g == HOT_PASSES - 1),
+                )
+
+        def whole_group(m, c, first=0, width=CHUNK):
+            tail_passes(m, c, first, width)
+            hot_passes(m, c, first, width)
+
+        def finish(m, c, first=0, width=CHUNK):
+            column = c * CHUNK + first
+            b, bank = open_groups[m, column]
+            t = stage.tile([P, width], F32, name="result_%d_%d" % (m, column), tag="result", bufs=RESULT_BUFS)
+            nc.vector.scalar_tensor_tensor(
+                out=t[:],
+                in0=bank[:, :width],
+                scalar=gain[:, m : m + 1],
+                in1=bias_sb[c][:, first : first + width],
+                op0=ALU.mult,
+                op1=ALU.add,
+            )
+            nc.sync.dma_start(out=out_rows[:, m, column : column + width], in_=t[:])
+            free_banks.append(b)
+
+        def warm_up(name, passes):
+            b, bank = take_bank(name)
+            codes, scales = z_mx[0, TAIL_SPANS[0]]
             for i in range(passes):
                 nc.tensor.matmul_mx(
                     out=bank[:, : 2 * P],
@@ -242,58 +302,54 @@ def tile_relu_dictionary_readout_s1_kernel(
                 )
             free_banks.append(b)
 
-        def hot_passes(m, c):
-            codes, scales = z_mx[m, HOT_SPAN]
-            for g in range(HOT_PASSES):
-                cols = slice(g * P, (g + 1) * P)
-                nc.tensor.matmul_mx(
-                    out=acc[m, c][:],
-                    lhsT=codes[:, cols].bitcast(FP8X4),
-                    lhsT_scale=scales[:, cols],
-                    rhs=hot_mx[c, g][0][:].bitcast(FP8X4),
-                    rhs_scale=hot_mx[c, g][1][:],
-                    start=False,
-                    stop=(g == HOT_PASSES - 1),
-                )
+        ident = keep.tile([P, P], F32, name="ident")
+        make_identity(nc, ident[:])
+        tail_planes = []
+        for c in range(CHUNKS):
+            plane = keep.tile([P, TAIL_PASSES, CHUNK], U8, name="tail_plane_%d" % c, align_bytes=MX_ALIGN)
+            nc.vector.memset(plane[:].bitcast(I32), 0)
+            tail_planes.append(plane)
+        theta_cols = keep.tile([P, SPANS, 8], BF16, name="theta_cols")
+        gain_raw = keep.tile([P, TILES], BF16, name="gain_raw")
+        bias_cols = keep.tile([P, CHUNKS, 4], BF16, name="bias_cols")
+        gain = keep.tile([P, TILES], F32, name="gain")
+        theta_quad = keep.tile([P, 2, 2, PASSES, QUAD], F32, name="theta_quad")
 
-        def finish(m, c, pieces=1):
-            width = CHUNK // pieces
-            for i in range(pieces):
-                cols = slice(i * width, (i + 1) * width)
-                t = stage.tile([P, width], F32, name="result_%d_%d_%d" % (m, c, i), tag="result", bufs=8)
-                nc.vector.scalar_tensor_tensor(
-                    out=t[:],
-                    in0=acc[m, c][:, cols],
-                    scalar=gain[:, m : m + 1],
-                    in1=bias_sb[c][:, cols],
-                    op0=ALU.mult,
-                    op1=ALU.add,
-                )
-                nc.sync.dma_start(out=out_rows[:, m, c * CHUNK + i * width : c * CHUNK + (i + 1) * width], in_=t[:])
-            free_banks.append(acc_bank[m, c])
+        nc.sync.dma_start(out=theta_cols[:], in_=theta.rearrange("(s p e) -> p s e", p=P, e=8))
+        load_pre(0, [1])
+        nc.sync.dma_start(out=gain_raw[:], in_=token_scale.rearrange("(p m) -> p m", m=TILES))
+        nc.sync.dma_start(out=bias_cols[:], in_=b_dec.rearrange("(c p e) -> p c e", p=P, e=4))
+        load_pre(0, [2])
+        load_pre(0, [0])
+        load_hot(0)
+        load_pre(1, [1, 2])
+        load_pre(1, [0])
+        load_tail(0)
+        load_tail(1)
+        load_hot(1)
+        load_pre(2, [1, 2])
+        load_pre(2, [0])
+        load_tail(2)
+        load_hot(2)
+        for m in (3, 4, 5):
+            load_pre(m, [0, 1, 2])
 
-        def both(m, c):
-            tail_passes(m, c)
-            hot_passes(m, c)
+        nc.scalar.activation(out=gain[:], in_=gain_raw[:], func=ACT.Identity)
 
-        vc = nc.vector.tensor_copy
-        sc = nc.scalar.copy
-        spread_theta(1, vc)
-        spread_theta(2, sc)
-        spread_theta(0, sc)
+        spread_theta(1, vector_copy)
+        spread_theta(2, scalar_copy)
+        spread_theta(0, scalar_copy)
         for c in range(CHUNKS):
             spread_bias(c)
-        subtract(0, 1)
-        subtract(0, 2)
-        subtract(0, 0)
-        turn_z(0, 1)
-        turn_z(0, 2)
-        turn_z(0, 0)
-        sort_hot(0, 0, vc)
+        for s in SPAN_ORDER:
+            subtract(0, s)
+        for s in SPAN_ORDER:
+            turn_z(0, s)
+        sort_hot(0, 0)
         quantize_z(0, 1)
-        sort_hot(0, 1, vc)
-        turn_hot(0, 0, [vc, sc])
-        warm_up(4)
+        sort_hot(0, 1)
+        turn_hot(0, 0, (vector_copy, scalar_copy))
+        warm_up("warm_early", 4)
         turn_hot(0, 1)
         quantize_z(0, 2)
         subtract(1, 1)
@@ -301,59 +357,59 @@ def tile_relu_dictionary_readout_s1_kernel(
         quantize_z(0, 0)
         subtract(1, 0)
         turn_z(1, 1)
-        turn_z(1, 2, True)
-        warm_up(2)
+        turn_z(1, 2, relu_on_vector)
+        warm_up("warm_late", 2)
         turn_z(1, 0)
-        quantize_hot(0, 0)
-        quantize_hot(0, 1)
-        both(0, 0)
-        quantize_z(1, 1)
-        quantize_z(1, 2)
-        quantize_z(1, 0)
+        quantize_hot(0)
+        whole_group(0, 0)
+        for s in SPAN_ORDER:
+            quantize_z(1, s)
         finish(0, 0)
-        both(1, 0)
-        sort_hot(1, 0, vc)
+        whole_group(1, 0)
+        gather_theta_quad()
+
+        sort_hot(1, 0)
         finish(1, 0)
-        sort_hot(1, 1, vc)
+        load_pre_quad(6, 0)
+        sort_hot(1, 1)
         tail_passes(0, 1)
-        turn_hot(1, 0)
-        turn_hot(1, 1)
-        subtract(2, 1)
-        subtract(2, 2)
-        subtract(2, 0)
+        for h in range(2):
+            turn_hot(1, h)
+        for s in SPAN_ORDER:
+            subtract(2, s)
         tail_passes(1, 1)
-        quantize_hot(1, 0)
-        quantize_hot(1, 1)
+        quantize_hot(1)
         turn_z(2, 1)
         turn_z(2, 2)
-        turn_z(2, 0, True)
+        turn_z(2, 0, relu_on_vector)
         tail_passes(0, 2)
         hot_passes(0, 1)
         hot_passes(1, 1)
         tail_passes(1, 2)
+
         quantize_z(2, 1)
-        sort_hot(2, 0, vc)
+        sort_hot(2, 0)
         quantize_z(2, 2)
-        sort_hot(2, 1, vc)
+        sort_hot(2, 1)
         quantize_z(2, 0)
         finish(0, 1)
         finish(1, 1)
-        turn_hot(2, 0)
-        turn_hot(2, 1)
-        subtract(3, 1)
-        subtract(3, 2)
-        subtract(3, 0)
-        both(2, 0)
-        both(2, 1)
-        quantize_hot(2, 0)
-        quantize_hot(2, 1)
+        load_pre_quad(6, 1)
+        for h in range(2):
+            turn_hot(2, h)
+        for s in SPAN_ORDER:
+            subtract(3, s)
+        whole_group(2, 0)
+        whole_group(2, 1)
+        quantize_hot(2)
         finish(2, 0)
-        for s in (1, 2, 0):
+        for s in SPAN_ORDER:
             turn_z(3, s)
         finish(2, 1)
+        load_pre_quad(7, 0)
         hot_passes(0, 2)
         hot_passes(1, 2)
-        both(2, 2)
+        whole_group(2, 2)
         subtract(4, 1)
         quantize_z(3, 1)
         subtract(4, 2)
@@ -361,27 +417,59 @@ def tile_relu_dictionary_readout_s1_kernel(
         quantize_z(3, 2)
         subtract(4, 0)
         finish(1, 2)
+        load_pre_quad(7, 1)
         quantize_z(3, 0)
 
-        for m in range(3, TILES):
-            turn = m + 1 < TILES
-            ahead = m + 2 < TILES
-            if turn:
-                for s in (1, 2, 0):
-                    turn_z(m + 1, s)
-            finish(m - 1, 2)
-            both(m, 0)
-            for s in TAIL_SPANS:
-                if ahead:
-                    subtract(m + 2, s)
-                if turn:
-                    quantize_z(m + 1, s)
-            finish(m, 0)
-            both(m, 1)
-            if turn:
-                quantize_z(m + 1, HOT_SPAN)
-            if ahead:
-                subtract(m + 2, HOT_SPAN)
-            finish(m, 1)
-            both(m, 2)
-        finish(TILES - 1, 2, 2)
+        for s in SPAN_ORDER:
+            turn_z(4, s)
+        finish(2, 2)
+        whole_group(3, 0)
+        for s in TAIL_SPANS:
+            subtract(5, s)
+            quantize_z(4, s)
+        finish(3, 0)
+        whole_group(3, 1)
+        subtract(5, HOT_SPAN)
+        quantize_z(4, HOT_SPAN)
+        finish(3, 1)
+        whole_group(3, 2)
+
+        subtract_quad(6, 0)
+        for s in SPAN_ORDER:
+            turn_z(5, s)
+        finish(3, 2)
+        turn_quad(6, 0)
+        whole_group(4, 0)
+        quantize_z(5, 1)
+        subtract_quad(6, 1)
+        quantize_z(5, 2)
+        turn_quad(6, 1)
+        finish(4, 0)
+        whole_group(4, 1)
+        quantize_z(5, 0)
+        finish(4, 1)
+        whole_group(4, 2)
+
+        subtract_quad(7, 0)
+        finish(4, 2)
+        whole_group(5, 0)
+        turn_quad(7, 0)
+        for s in SPAN_ORDER:
+            quantize_z(6, s)
+        subtract_quad(7, 1)
+        finish(5, 0)
+        turn_quad(7, 1)
+        for c in (1, 2):
+            whole_group(5, c)
+            finish(5, c)
+
+        whole_group(6, 0)
+        for s in SPAN_ORDER:
+            quantize_z(7, s)
+        finish(6, 0)
+        for m, c in ((6, 1), (6, 2), (7, 0), (7, 1)):
+            whole_group(m, c)
+            finish(m, c)
+        for first in range(0, CHUNK, P):
+            whole_group(7, 2, first, P)
+            finish(7, 2, first, P)

@@ -287,21 +287,6 @@ def tile_relu_dictionary_readout_s1_kernel(
             nc.sync.dma_start(out=out_rows[:, m, column : column + width], in_=t[:])
             free_banks.append(b)
 
-        def warm_up(name, passes):
-            b, bank = take_bank(name)
-            codes, scales = z_mx[0, TAIL_SPANS[0]]
-            for i in range(passes):
-                nc.tensor.matmul_mx(
-                    out=bank[:, : 2 * P],
-                    lhsT=codes[:, :P].bitcast(FP8X4),
-                    lhsT_scale=scales[:, :P],
-                    rhs=codes[:].bitcast(FP8X4),
-                    rhs_scale=scales[:],
-                    start=True,
-                    stop=True,
-                )
-            free_banks.append(b)
-
         ident = keep.tile([P, P], F32, name="ident")
         make_identity(nc, ident[:])
         tail_planes = []
@@ -349,7 +334,6 @@ def tile_relu_dictionary_readout_s1_kernel(
         quantize_z(0, 1)
         sort_hot(0, 1)
         turn_hot(0, 0, (vector_copy, scalar_copy))
-        warm_up("warm_early", 4)
         turn_hot(0, 1)
         quantize_z(0, 2)
         subtract(1, 1)
@@ -358,7 +342,6 @@ def tile_relu_dictionary_readout_s1_kernel(
         subtract(1, 0)
         turn_z(1, 1)
         turn_z(1, 2, relu_on_vector)
-        warm_up("warm_late", 2)
         turn_z(1, 0)
         quantize_hot(0)
         whole_group(0, 0)

from contextlib import ExitStack

import concourse.mybir as mybir
from concourse.masks import make_identity

M, H, T, N = 1024, 1024, 2048, 1536
FLOPS = 2 * M * (H + T) * N

F32 = mybir.dt.float32
BF16 = mybir.dt.bfloat16
I32 = mybir.dt.int32
U32 = mybir.dt.uint32
U8 = mybir.dt.uint8
FP8X4 = mybir.dt.float8_e4m3fn_x4
FP4X4 = mybir.dt.float4_e2m1fn_x4
ALU = mybir.AluOpType
ACT = mybir.ActivationFunctionType

P = 128
BANKS = 8
QUAD = 32
QUADS = P // QUAD
TILES = M // P
CHUNK = 512
CHUNKS = N // CHUNK
SPAN = 1024
SPANS = (H + T) // SPAN
HOT_SPAN = 0
TAIL_SPANS = (1, 2)
SPAN_ORDER = (1, 2, 0)
HOT_PASSES = H // 512
TAIL_PASSES = T // 512
PASSES = HOT_PASSES + TAIL_PASSES
MX_ALIGN = 64

DIFF_BUFS = 2 * SPANS
TURNED_BUFS = SPANS + 1
RESULT_BUFS = 9


def tile_relu_dictionary_readout_s1_kernel(
    tc, pre, theta, hot, tail_words, tail_scales, token_scale, b_dec, out
):
    nc = tc.nc
    vector_copy, scalar_copy = nc.vector.tensor_copy, nc.scalar.copy
    pre_rows = pre.rearrange("(p m) k -> p m k", m=TILES)
    out_rows = out.rearrange("(p m) n -> p m n", m=TILES)
    hot_rows = hot.rearrange("(c h j p) k -> c h p j k", h=2, j=2, p=P)
    tail_by_partition = tail_words.rearrange("g p n -> p g n")

    with ExitStack() as ctx:
        keep = ctx.enter_context(tc.tile_pool(name="keep", bufs=1))
        stage = ctx.enter_context(tc.tile_pool(name="stage", bufs=2))
        psum = ctx.enter_context(tc.psum_pool(name="psum", bufs=1))
        ctx.enter_context(tc.manual_schedule())

        pre_sb, diff, z_turned, z_mx = {}, {}, {}, {}
        pre_quad, diff_quad = {}, {}
        z_quad = {}
        hot_sb, hot_sorted = {}, {}
        hot_turned, hot_mx = {}, {}
        tail_sb, bias_sb = {}, {}
        theta_sb = {}
        open_groups = {}

        free_banks = list(range(BANKS))

        def take_bank(name):
            b = free_banks.pop(0)
            return b, psum.tile([P, CHUNK], F32, name=name, tag="bank_%d" % b)

        def load_pre(m, spans):
            t = keep.tile([P, len(spans) * SPAN], BF16, name="pre_%d_%d" % (m, spans[0]))
            nc.sync.dma_start(out=t[:], in_=pre_rows[:, m, spans[0] * SPAN : (spans[-1] + 1) * SPAN])
            for i, s in enumerate(spans):
                pre_sb[m, s] = t[:, i * SPAN : (i + 1) * SPAN]

        def load_pre_quad(m, h):
            rows = pre_rows[:, m, :].rearrange("(a i) (g q k) -> q a i g k", i=QUAD, q=QUADS, k=P)
            t = keep.tile([P, 2, PASSES, P], BF16, name="pre_quad_%d_%d" % (m, h))
            for a in range(2):
                for q in (0, 2, 1, 3):
                    nc.sync.dma_start(out=t[QUAD * q : QUAD * (q + 1), a], in_=rows[q, 2 * h + a])
            pre_quad[m, h] = t

        def load_hot(c):
            for h in range(2):
                t = keep.tile([P, 2, H], BF16, name="hot_%d_%d" % (c, h))
                nc.sync.dma_start(out=t[:], in_=hot_rows[c, h])
                hot_sb[c, h] = t

        def load_tail(c):
            for q in range(QUADS):
                nc.sync.dma_start(
                    out=tail_planes[c][QUAD * q : QUAD * q + 4].bitcast(I32),
                    in_=tail_scales[:, 4 * q : 4 * q + 4, c * CHUNK : (c + 1) * CHUNK]
                    .rearrange("g r n -> r g n")
                    .bitcast(I32),
                )
            t = keep.tile([P, TAIL_PASSES, 2 * CHUNK], U8, name="tail_%d" % c, align_bytes=MX_ALIGN)
            nc.sync.dma_start(
                out=t[:].bitcast(I32),
                in_=tail_by_partition[:, :, 2 * CHUNK * c : 2 * CHUNK * (c + 1)].bitcast(I32),
            )
            tail_sb[c] = t

        def spread_theta(s, copy):
            b, bank = take_bank("theta_bank_%d" % s)
            pairs = theta_cols[:, s, :].bitcast(F32)
            for w in range(4):
                nc.tensor.transpose(bank[:, w * P : (w + 1) * P], pairs[:, w : w + 1].to_broadcast([P, P]), ident[:])
            t = keep.tile([P, SPAN], BF16, name="theta_%d" % s)
            copy(
                out=t[:].bitcast(F32).rearrange("p (u n v) -> p u n v", u=2, v=2),
                in_=bank[:].rearrange("p (v u n) -> p u n v", u=2, v=2),
            )
            theta_sb[s] = t
            free_banks.append(b)

        def spread_bias(c):
            b, bank = take_bank("bias_bank_%d" % c)
            pairs = bias_cols[:, c, :].bitcast(F32)
            for w in range(2):
                nc.tensor.transpose(bank[:, w * P : (w + 1) * P], pairs[:, w : w + 1].to_broadcast([P, P]), ident[:])
            t = keep.tile([P, CHUNK], BF16, name="bias_%d" % c)
            scalar_copy(
                out=t[:].bitcast(F32).rearrange("p (n w) -> p n w", w=2),
                in_=bank[:, : 2 * P].rearrange("p (w n) -> p n w", w=2),
            )
            bias_sb[c] = t
            free_banks.append(b)

        def gather_theta_quad():
            for q in range(QUADS):
                rows = slice(QUAD * q, QUAD * (q + 1))
                for s in range(SPANS):
                    pairs = theta_sb[s][rows].bitcast(F32).rearrange("p (u g q j) -> p u g q j", u=2, g=2, q=QUADS)
                    scalar_copy(out=theta_quad[rows, :, 0, 2 * s : 2 * s + 2, :], in_=pairs[:, :, :, q, :])
            scalar_copy(out=theta_quad[:, :, 1], in_=theta_quad[:, :, 0])

        def subtract(m, s):
            t = stage.tile([P, SPAN], BF16, name="diff_%d_%d" % (m, s), tag="diff", bufs=DIFF_BUFS)
            nc.vector.tensor_tensor(
                out=t[:].rearrange("p (u w e) -> p u w e", u=2, e=2),
                in0=pre_sb[m, s].rearrange("p (w u e) -> p u w e", u=2, e=2),
                in1=theta_sb[s][:].rearrange("p (u w e) -> p u w e", u=2, e=2),
                op=ALU.subtract,
            )
            diff[m, s] = t

        def relu_on_scalar(target, source):
            nc.scalar.activation(out=target, in_=source, func=ACT.Relu)

        def relu_on_vector(target, source):
            nc.vector.tensor_scalar_max(target, source, 0.0)

        def turn_z(m, s, relu=relu_on_scalar):
            b, bank = take_bank("z_bank_%d_%d" % (m, s))
            pairs = diff[m, s][:].bitcast(F32)
            for i in range(4):
                nc.tensor.transpose(bank[:, i * P : (i + 1) * P], pairs[:, i * P : (i + 1) * P], ident[:])
            t = stage.tile(
                [P, SPAN], BF16, name="z_turned_%d_%d" % (m, s), tag="z_turned", bufs=TURNED_BUFS, align_bytes=MX_ALIGN
            )
            relu(
                t[:].rearrange("p (r u e) -> p r u e", u=2, e=2),
                bank[:].bitcast(BF16).rearrange("p (u r e) -> p r u e", u=2, e=2),
            )
            z_turned[m, s] = t[:]
            free_banks.append(b)

        def quantize_z(m, s):
            codes = keep.tile([P, 2 * P], U32, name="z_codes_%d_%d" % (m, s), align_bytes=MX_ALIGN)
            scales = keep.tile([P, 2 * P], U8, name="z_scales_%d_%d" % (m, s), align_bytes=MX_ALIGN)
            nc.vector.quantize_mx(out=codes[:].bitcast(FP8X4), scales=scales[:], in_=z_turned[m, s])
            z_mx[m, s] = (codes, scales)

        def subtract_quad(m, h):
            t = stage.tile(
                [P, 2 * PASSES * P], BF16, name="diff_quad_%d_%d" % (m, h), tag="diff_quad", align_bytes=MX_ALIGN
            )
            nc.vector.tensor_tensor(
                out=t[:].rearrange("p (u a w e) -> p u a w e", u=2, a=2, e=2),
                in0=pre_quad[m, h][:].rearrange("p a g (j u e) -> p u a (g j) e", u=2, e=2),
                in1=theta_quad[:].bitcast(BF16).rearrange("p u a g (j e) -> p u a (g j) e", e=2),
                op=ALU.subtract,
            )
            diff_quad[m, h] = t

        def turn_quad(m, h):
            blocks = stage.tile(
                [P, PASSES * P], F32, name="blocks_%d_%d" % (m, h), tag="blocks", align_bytes=MX_ALIGN
            )
            nc.vector.transpose(blocks[:], diff_quad[m, h][:].bitcast(F32))
            if h == 0:
                z_quad[m] = stage.tile(
                    [P, SPANS * SPAN], BF16, name="z_quad_%d" % m, tag="z_quad", align_bytes=MX_ALIGN
                )
                for s in range(SPANS):
                    z_turned[m, s] = z_quad[m][:, s * SPAN : (s + 1) * SPAN]
            by_token_group = z_quad[m][:].rearrange("p (g a i u e) -> p a g i u e", a=QUADS, i=QUAD, u=2, e=2)
            relu_on_scalar(
                by_token_group[:, 2 * h : 2 * h + 2],
                blocks[:].bitcast(BF16).rearrange("p (u a g i e) -> p a g i u e", u=2, a=2, i=QUAD, e=2),
            )

        def sort_hot(c, h):
            t = stage.tile([P, 2, 2, 2 * P], F32, name="hot_sorted_%d_%d" % (c, h), tag="hot_sorted")
            vector_copy(out=t[:], in_=hot_sb[c, h][:].bitcast(F32).rearrange("p j (w u) -> p j u w", u=2))
            hot_sorted[c, h] = t

        def turn_hot(c, h, copies=(scalar_copy, scalar_copy)):
            for g in range(HOT_PASSES):
                if h == 0:
                    hot_turned[c, g] = stage.tile(
                        [P, 4 * CHUNK], BF16, name="hot_turned_%d_%d" % (c, g), tag="hot_turned", align_bytes=MX_ALIGN
                    )
                b, bank = take_bank("hot_bank_%d_%d_%d" % (c, h, g))
                for u in range(2):
                    for j in range(2):
                        i = 2 * u + j
                        nc.tensor.transpose(
                            bank[:, i * P : (i + 1) * P], hot_sorted[c, h][:, j, u, g * P : (g + 1) * P], ident[:]
                        )
                half = hot_turned[c, g][:, 2 * CHUNK * h : 2 * CHUNK * (h + 1)]
                copies[g](
                    out=half.bitcast(F32).rearrange("p (r u) -> p r u", u=2),
                    in_=bank[:].rearrange("p (u r) -> p r u", u=2),
                )
                free_banks.append(b)

        def quantize_hot(c):
            for g in range(HOT_PASSES):
                codes = keep.tile([P, CHUNK], U32, name="hot_codes_%d_%d" % (c, g), align_bytes=MX_ALIGN)
                scales = keep.tile([P, CHUNK], U8, name="hot_scales_%d_%d" % (c, g), align_bytes=MX_ALIGN)
                nc.vector.quantize_mx(out=codes[:].bitcast(FP8X4), scales=scales[:], in_=hot_turned[c, g][:])
                hot_mx[c, g] = (codes, scales)

        def tail_passes(m, c, first=0, width=CHUNK):
            open_groups[m, c * CHUNK + first] = take_bank("sums_%d_%d" % (m, c * CHUNK + first))
            bank = open_groups[m, c * CHUNK + first][1]
            for g in range(TAIL_PASSES):
                codes, scales = z_mx[m, TAIL_SPANS[g // 2]]
                tokens = slice((g % 2) * P, (g % 2 + 1) * P)
                nc.tensor.matmul_mx(
                    out=bank[:, :width],
                    lhsT=codes[:, tokens].bitcast(FP8X4),
                    lhsT_scale=scales[:, tokens],
                    rhs=tail_sb[c][:, g, 2 * first : 2 * (first + width)].bitcast(FP4X4),
                    rhs_scale=tail_planes[c][:, g, first : first + width],
                    start=(g == 0),
                    stop=False,
                )

        def hot_passes(m, c, first=0, width=CHUNK):
            bank = open_groups[m, c * CHUNK + first][1]
            codes, scales = z_mx[m, HOT_SPAN]
            for g in range(HOT_PASSES):
                tokens = slice(g * P, (g + 1) * P)
                hot_codes, hot_scales = hot_mx[c, g]
                nc.tensor.matmul_mx(
                    out=bank[:, :width],
                    lhsT=codes[:, tokens].bitcast(FP8X4),
                    lhsT_scale=scales[:, tokens],
                    rhs=hot_codes[:, first : first + width].bitcast(FP8X4),
                    rhs_scale=hot_scales[:, first : first + width],
                    start=False,
                    stop=(g == HOT_PASSES - 1),
                )

        def whole_group(m, c, first=0, width=CHUNK):
            tail_passes(m, c, first, width)
            hot_passes(m, c, first, width)

        def finish(m, c, first=0, width=CHUNK):
            column = c * CHUNK + first
            b, bank = open_groups[m, column]
            t = stage.tile([P, width], F32, name="result_%d_%d" % (m, column), tag="result", bufs=RESULT_BUFS)
            nc.vector.scalar_tensor_tensor(
                out=t[:],
                in0=bank[:, :width],
                scalar=gain[:, m : m + 1],
                in1=bias_sb[c][:, first : first + width],
                op0=ALU.mult,
                op1=ALU.add,
            )
            nc.sync.dma_start(out=out_rows[:, m, column : column + width], in_=t[:])
            free_banks.append(b)

        ident = keep.tile([P, P], F32, name="ident")
        make_identity(nc, ident[:])
        tail_planes = []
        for c in range(CHUNKS):
            plane = keep.tile([P, TAIL_PASSES, CHUNK], U8, name="tail_plane_%d" % c, align_bytes=MX_ALIGN)
            nc.vector.memset(plane[:].bitcast(I32), 0)
            tail_planes.append(plane)
        theta_cols = keep.tile([P, SPANS, 8], BF16, name="theta_cols")
        gain_raw = keep.tile([P, TILES], BF16, name="gain_raw")
        bias_cols = keep.tile([P, CHUNKS, 4], BF16, name="bias_cols")
        gain = keep.tile([P, TILES], F32, name="gain")
        theta_quad = keep.tile([P, 2, 2, PASSES, QUAD], F32, name="theta_quad")

        nc.sync.dma_start(out=theta_cols[:], in_=theta.rearrange("(s p e) -> p s e", p=P, e=8))
        load_pre(0, [1])
        nc.sync.dma_start(out=gain_raw[:], in_=token_scale.rearrange("(p m) -> p m", m=TILES))
        nc.sync.dma_start(out=bias_cols[:], in_=b_dec.rearrange("(c p e) -> p c e", p=P, e=4))
        load_pre(0, [2])
        load_pre(0, [0])
        load_hot(0)
        load_pre(1, [1, 2])
        load_pre(1, [0])
        load_tail(0)
        load_tail(1)
        load_hot(1)
        load_pre(2, [1, 2])
        load_pre(2, [0])
        load_tail(2)
        load_hot(2)
        for m in (3, 4, 5):
            load_pre(m, [0, 1, 2])

        nc.scalar.activation(out=gain[:], in_=gain_raw[:], func=ACT.Identity)

        spread_theta(1, vector_copy)
        spread_theta(2, scalar_copy)
        spread_theta(0, scalar_copy)
        for c in range(CHUNKS):
            spread_bias(c)
        for s in SPAN_ORDER:
            subtract(0, s)
        for s in SPAN_ORDER:
            turn_z(0, s)
        sort_hot(0, 0)
        quantize_z(0, 1)
        sort_hot(0, 1)
        turn_hot(0, 0, (vector_copy, scalar_copy))
        turn_hot(0, 1)
        quantize_z(0, 2)
        subtract(1, 1)
        subtract(1, 2)
        quantize_z(0, 0)
        subtract(1, 0)
        turn_z(1, 1)
        turn_z(1, 2, relu_on_vector)
        turn_z(1, 0)
        quantize_hot(0)
        whole_group(0, 0)
        for s in SPAN_ORDER:
            quantize_z(1, s)
        finish(0, 0)
        whole_group(1, 0)
        gather_theta_quad()

        sort_hot(1, 0)
        finish(1, 0)
        load_pre_quad(6, 0)
        sort_hot(1, 1)
        tail_passes(0, 1)
        for h in range(2):
            turn_hot(1, h)
        for s in SPAN_ORDER:
            subtract(2, s)
        tail_passes(1, 1)
        quantize_hot(1)
        turn_z(2, 1)
        turn_z(2, 2)
        turn_z(2, 0, relu_on_vector)
        tail_passes(0, 2)
        hot_passes(0, 1)
        hot_passes(1, 1)
        tail_passes(1, 2)

        quantize_z(2, 1)
        sort_hot(2, 0)
        quantize_z(2, 2)
        sort_hot(2, 1)
        quantize_z(2, 0)
        finish(0, 1)
        finish(1, 1)
        load_pre_quad(6, 1)
        for h in range(2):
            turn_hot(2, h)
        for s in SPAN_ORDER:
            subtract(3, s)
        whole_group(2, 0)
        whole_group(2, 1)
        quantize_hot(2)
        finish(2, 0)
        for s in SPAN_ORDER:
            turn_z(3, s)
        finish(2, 1)
        load_pre_quad(7, 0)
        hot_passes(0, 2)
        hot_passes(1, 2)
        whole_group(2, 2)
        subtract(4, 1)
        quantize_z(3, 1)
        subtract(4, 2)
        finish(0, 2)
        quantize_z(3, 2)
        subtract(4, 0)
        finish(1, 2)
        load_pre_quad(7, 1)
        quantize_z(3, 0)

        for s in SPAN_ORDER:
            turn_z(4, s)
        finish(2, 2)
        whole_group(3, 0)
        for s in TAIL_SPANS:
            subtract(5, s)
            quantize_z(4, s)
        finish(3, 0)
        whole_group(3, 1)
        subtract(5, HOT_SPAN)
        quantize_z(4, HOT_SPAN)
        finish(3, 1)
        whole_group(3, 2)

        subtract_quad(6, 0)
        for s in SPAN_ORDER:
            turn_z(5, s)
        finish(3, 2)
        turn_quad(6, 0)
        whole_group(4, 0)
        quantize_z(5, 1)
        subtract_quad(6, 1)
        quantize_z(5, 2)
        turn_quad(6, 1)
        finish(4, 0)
        whole_group(4, 1)
        quantize_z(5, 0)
        finish(4, 1)
        whole_group(4, 2)

        subtract_quad(7, 0)
        finish(4, 2)
        whole_group(5, 0)
        turn_quad(7, 0)
        for s in SPAN_ORDER:
            quantize_z(6, s)
        subtract_quad(7, 1)
        finish(5, 0)
        turn_quad(7, 1)
        for c in (1, 2):
            whole_group(5, c)
            finish(5, c)

        whole_group(6, 0)
        for s in SPAN_ORDER:
            quantize_z(7, s)
        finish(6, 0)
        for m, c in ((6, 1), (6, 2), (7, 0), (7, 1)):
            whole_group(m, c)
            finish(m, c)
        for first in range(0, CHUNK, P):
            whole_group(7, 2, first, P)
            finish(7, 2, first, P)
